import numpy as np, ml_dtypes
CORES = [9,25,41,57]
N = 4
BF = ml_dtypes.bfloat16
def gentries(a):
    return np.ascontiguousarray(a.reshape(8, 16, -1).transpose(0, 2, 1)).reshape(8, -1)
def gtable(e):
    e = np.asarray(e); return np.ascontiguousarray(e.reshape(8, -1, 16).transpose(0, 2, 1)).reshape(128, -1).astype(np.int32)
V, R, L, S = 4096, 256, 4, 2
def trees(rng, deep):
    T = N * 8; ar = np.arange(T); P = V // 2 - 1; i = np.arange(P)[:, None]
    pair = 2 * (np.argsort(rng.random((T, P)), axis=1) + 1); side = rng.integers(0, 2, (P, T))
    pick = np.where(rng.random((P, T)) < deep, i, np.minimum((rng.random((P, T)) * (i + 1)).astype(np.int64), i))
    kid = np.full((T, V), -1, np.int64); up = np.zeros((T, V), np.int64); leaf = np.zeros((T, P + 1), np.int64); cnt = np.ones((T, V), np.int64)
    for t in range(P):
        j = pick[t]; n = leaf[ar, j]; k = pair[:, t]; b = side[t]
        kid[ar, n] = k; up[ar, k] = n; up[ar, k + 1] = n
        leaf[ar, j] = k + b; leaf[ar, t + 1] = k + 1 - b
    for t in range(P - 1, -1, -1):
        k = pair[:, t]; cnt[ar, up[ar, k]] = cnt[ar, k] + cnt[ar, k + 1]
    return kid, up, cnt
def quads(rng, kid, cnt, top, drop):
    T = N * 8; Q = 4 * R; ar = np.arange(T)[:, None]; ar3 = ar[:, :, None]
    ok = cnt >= 4; order = np.argsort(~ok, axis=1, kind="stable"); num = np.sum(ok, axis=1)[:, None]
    x = order[ar, np.minimum((rng.random((T, Q)) * num).astype(np.int64), num - 1)]
    c = np.full((T, Q, 4), -1, np.int64); c[:, :, 0] = np.where(rng.random((T, Q)) < top, 0, x)
    for w in (1, 2, 3):
        k = kid[ar3, np.maximum(c, 0)]
        t = np.argmax(np.where((c >= 0) & (k >= 0), rng.random(c.shape), -1.0), axis=2)[..., None]
        k = np.take_along_axis(k, t, 2); np.put_along_axis(c, t, k, 2); c[:, :, w] = k[..., 0] + 1
    m = rng.random((T, Q, 1)) < drop
    for w in range(4):
        k = kid[ar3, c]; go = m & (k >= 0) & (rng.random(c.shape) < 0.3)
        c = np.where(go, k + rng.integers(0, 2, c.shape), c)
    return np.take_along_axis(c, np.argsort(rng.random(c.shape), axis=2), 2)
def parts(rng, deep=0.2, top=0.15, drop=0.5):
    kid, up, cnt = trees(rng, deep)
    return {"s": rng.integers(0, 256, (N, 8, 16, V)), "m": rng.integers(0, 256, (N, 8, 16, V)), "kid": kid, "up": up,
            "a": rng.integers(0, 256, (N, 8, 16, R)), "a0": rng.integers(0, 256, (N, 8, 16, R)), "lk": rng.integers(0, R, (N, 8, L, R)), "cut0": quads(rng, kid, cnt, top, drop)}
def pack(d):
    q = {}
    for k in ("s", "m", "kid", "up", "a", "a0", "lk", "cut0"):
        v = d[k]
        if k in ("kid", "up"): q[k] = np.ascontiguousarray(v.reshape(N, 8, V)).astype(np.int32)
        elif k in ("lk", "cut0"): q[k] = np.stack([gtable(x) for x in v.reshape(N, 8, -1)])
        else: q[k] = np.ascontiguousarray(v.reshape(N, 128, -1)).astype(np.float32).astype(BF)
    return q
def setup_inputs(rng):
    return pack(parts(rng))
def setup_inputs_ties(rng):
    d = parts(rng, 0.2, 0.3, 0.4)
    d["a"] = rng.integers(1, 3, (N, 8, 16, R)); d["a0"] = rng.integers(1, 3, (N, 8, 16, R))
    d["s"] = np.repeat(rng.integers(0, 3, (N, 8, 1, V)) * rng.choice(np.array([1, 7, 100]), (N, 8, 1, 1)), 16, axis=2)
    d["s"][:, 3] = 7; d["s"][:, 5] = np.where(rng.random((N, 16, V)) < 0.5, 1, 2)
    return pack(d)
def setup_inputs_deep(rng):
    T = N * 8; Q = 4 * R; deep = rng.choice(np.array([0.0, 0.9, 1.0]), (1, T)); deep[0, 0] = 1.0; deep[0, T - 1] = 0.0
    d = parts(rng, deep, 0.05, 0.3); n = np.arange(V)[None, :]
    leaf = np.argsort(np.where((d["kid"] < 0) & (n != 1), n, V + n), axis=1)[:, :V // 2]
    at = rng.integers(0, V // 2 - 3, (T, Q)); at[:, 0] = 0; at[:, 1] = V // 2 - 4
    m = rng.random((T, Q)) < 0.4; m[:, :2] = True
    four = leaf[np.arange(T)[:, None, None], at[:, :, None] + np.arange(4)]
    four = np.take_along_axis(four, np.argsort(rng.random(four.shape), axis=2), 2)
    d["cut0"] = np.where(m[:, :, None], four, d["cut0"])
    return pack(d)
def top_end(rng, d, g):
    ar = np.arange(N); c = d["cut0"].reshape(N, 8, R, 4, 4).copy(); k = d["kid"].reshape(N, 8, V)[:, g]; u = d["up"].reshape(N, 8, V)[:, g]
    q = c[:, g].reshape(N, 4 * R, 4); sib = np.any(q[..., None, :] == (q ^ 1)[..., :, None], axis=3)
    q = np.take_along_axis(q, np.argsort(~sib, axis=2, kind="stable"), 2)
    inner = k[ar[:, None, None], q] >= 0; good = (np.sum(sib, axis=2) == 2) & inner[..., 2] & inner[..., 3]
    p = q[ar, np.argmax(good, axis=1)]
    c[:, g] = q.reshape(N, R, 4, 4); c[:, g, ::2, 0] = p[:, None, :]; d["cut0"] = c
    j = rng.integers(0, 16, (N, V))
    j[ar, p[:, 0]] = 2; j[ar, p[:, 1]] = 2; j[ar, u[ar, p[:, 0]]] = 2; j[ar, p[:, 2]] = 1; j[ar, p[:, 3]] = 1
    d["s"][:, g] = 255 - (np.arange(16)[None, :, None] == j[:, None, :]).astype(np.int64)
    d["a"][:, g] = rng.integers(254, 256, (N, 16, R)); d["a"][:, g, 12:] = 255; d["a"][:, g, 1, ::2] = 254; d["a"][:, g, 2, ::2] = 255
    d["a0"][:, g] = rng.integers(0, 2, (N, 16, R))
def setup_inputs_ends(rng):
    d = parts(rng)
    for k in ("s", "m", "a", "a0"):
        e = rng.random(d[k].shape); d[k] = np.where(e < 0.4, 255, np.where(e < 0.7, 0, d[k]))
    for k in ("s", "m", "a"): d[k][:, 0] = 255
    d["a"][:, 1, :, ::2] = 0; d["s"][:, 2] = 0
    d["lk"][:, ::2] = rng.choice(np.array([0, R - 1]), (N, 4, L, R))
    top_end(rng, d, 7)
    return pack(d)
def setup_inputs_alike(rng):
    d = parts(rng, 0.0, 1.0, 0.2)
    d["lk"][:, 1::2] = rng.integers(0, R, (N, 4, 1, 1))
    c = d["cut0"].reshape(N, 8, R, 16).copy(); c[:, ::2] = c[:, ::2, :1].copy(); d["cut0"] = c
    d["a"][:, :4] = np.repeat(d["a"][:, :4, :, :R // 16], 16, axis=3); d["a0"][:, 2:6, :, :R // 2] = d["a"][:, 2:6, :, :R // 2]
    return pack(d)
def setup_inputs_spread(rng):
    d = parts(rng)
    for k in ("s", "m", "a", "a0"):
        n = d[k].shape[3]; d[k] = np.floor(np.exp2(8 * rng.random((N, 8, 1, n))) * rng.random((N, 8, 16, n))).astype(np.int64)
    return pack(d)
def check_inputs(d):
    bad = []
    for k in ("s", "m", "a", "a0"):
        x = np.asarray(d[k]).astype(np.float32)
        if not np.all((x >= 0) & (x <= 255) & (x == np.floor(x))): bad.append("numbers of " + k)
    if np.min(d["lk"]) < 0 or np.max(d["lk"]) > R - 1: bad.append("range of lk")
    if np.min(d["cut0"]) < 2 or np.max(d["cut0"]) > V - 1: bad.append("range of cut0")
    T = N * 8; kid = np.asarray(d["kid"]).astype(np.int64).reshape(T, V); up = np.asarray(d["up"]).astype(np.int64).reshape(T, V)
    if np.min(kid) < -1 or np.max(kid) > V - 1 or np.min(up) < 0 or np.max(up) > V - 1: return bad + ["range of the trees"]
    ar = np.arange(T)[:, None]; n = np.arange(V)[None, :]
    ok = np.all(up[:, :2] == 0) and np.all(kid[:, 1] == -1) and np.all((kid == -1) | ((kid >= 2) & (kid % 2 == 0)))
    ok = ok and np.all(kid[ar, up][:, 2:] == (n - n % 2)[:, 2:]) and np.all(up[:, 0::2] == up[:, 1::2])
    ok = ok and np.all((kid < 0) | (up[ar, np.maximum(kid, 0)] == n))
    jump = [up]; dep = np.where(n == 0, 0, 1) + np.zeros((T, 1), np.int64); K = V.bit_length()
    for k in range(K):
        dep = dep + dep[ar, jump[-1]]; jump.append(jump[-1][ar, jump[-1]])
    if not ok or np.any(jump[-1]): return bad + ["trees"]
    if "range of cut0" in bad: return bad
    c = np.stack([gentries(np.asarray(x)) for x in d["cut0"]]).astype(np.int64).reshape(T, 4 * R, 4); wrong = False
    for i in range(4):
        for j in range(i):
            x, y = c[:, :, i], c[:, :, j]; dx, dy = dep[ar, x], dep[ar, y]
            low = np.where(dx >= dy, x, y); high = np.where(dx >= dy, y, x); dif = np.abs(dx - dy)
            for k in range(K): low = np.where(((dif >> k) & 1) > 0, jump[k][ar, low], low)
            wrong = wrong or bool(np.any(low == high))
    if wrong: bad.append("quads of cut0")
    return bad
def reference(s, m, kid, up, a, a0, lk, cut0):
    def rows(x, n): return np.ascontiguousarray(x.astype(np.float32).astype(np.int64).reshape(N, 8, 16, n).transpose(0, 1, 3, 2))
    sv, mv, av, ka = rows(s, V), rows(m, V), rows(a, R), rows(a0, R)
    kd, pu = kid.astype(np.int64), up.astype(np.int64)
    lv = np.stack([gentries(x) for x in lk]).astype(np.int64).reshape(N, 8, L, R)
    cut = np.stack([gentries(x) for x in cut0]).astype(np.int64).reshape(N, 8, R, 4, 4)
    G3 = np.arange(8)[:, None, None]; G4 = G3[..., None]; E = np.zeros((N, 8, R, 16), np.int64)
    def at(x, i): return np.take_along_axis(x, i, 3)
    for h in range(N):
        newcut = []; newa = []
        for r in range(N):
            b = (r - h) % N; x = av[b]; w = lv[b]
            dist = np.sum(np.abs(x[:, None] - ka[r][G3, w]).reshape(8, L, R, 4, 4), axis=4)
            best = np.argmin(dist, axis=1)
            own = w[G3, best, np.arange(R)[None, :, None]]
            c = cut[r][G3, own, np.arange(4)[None, None, :]]
            xx = x[:, :, None, None, :]
            for step in range(S):
                k = kd[r][G4, c]; p = pu[r][G4, c]
                err = np.where(k >= 0, np.sum(sv[r][G4, c] * xx, axis=4), -1)
                cost = np.sum(sv[r][G4, p] * xx, axis=4)
                i = np.argmax(err, axis=3)[..., None]; free = np.arange(4) != i
                mate = (c[..., None, :] == (c ^ 1)[..., :, None]) & free[..., None, :] & free[..., :, None]
                pair = np.any(mate, axis=4); j = np.argmax(pair, axis=3)[..., None]
                j2 = np.argmax(np.take_along_axis(mate, j[..., None], 3)[..., 0, :], axis=3)[..., None]
                go = np.any(pair, axis=3)[..., None] & (at(cost, j) < at(err, i)); left = at(k, i)
                new = c.copy()
                np.put_along_axis(new, i, left, 3); np.put_along_axis(new, j, at(p, j), 3); np.put_along_axis(new, j2, left + 1, 3)
                c = np.where(go, new, c)
            E[b] += x * np.sum(mv[r][G4, c], axis=(2, 3))
            newcut.append(c); newa.append(x)
        cut = np.stack(newcut); ka = np.stack(newa)
    return {"ye": np.ascontiguousarray(E.transpose(0, 1, 3, 2)).reshape(N, 128, R).astype(np.float32), "yc": np.stack([gtable(x.reshape(8, -1)) for x in cut]).astype(np.float32)}

from concourse.bass import DstId, RemoteDMATransfer
from concourse.mybir import AluOpType, ActivationFunctionType

OP = AluOpType
AF = ActivationFunctionType
BIG = 8388608.0

_W = {}
_n = [0]
for _k in "ups yd16 lab lbk kes o prk prl prr lt s1 s2 n0 n1 n2".split():
    _W[_k] = (_n[0], 128); _n[0] += 128
for _k in "eq peq xa na mab nab w1 w0 sab t1 tl tr u1 u2 u3 y1 y2 y3 mk lbf z zc".split():
    _W[_k] = (_n[0], 64); _n[0] += 64
for _k in ("pa pb ga gb ka kb ja jb pa2 pb2 lj ljp upu sib hasp mx mn ljm ljq ls lp mxm mn1 aa bb dz zr1 dab dr "
           "fk0 fk2 fk3 d0 d1 kl kr mxu g1a k2 sl g1 gs b1 b2 bbb m0 e1 e2 e3 go2 m1").split():
    _W[_k] = (_n[0], 32); _n[0] += 32

SCRATCH = {
    "kl": ("sbuf", [128, 256], "int32"), "ul": ("sbuf", [128, 256], "int32"),
    "ytk": ("sbuf", [128, 256], "int32"), "ytu": ("sbuf", [128, 256], "int32"),
    "xk": ("sbuf", [128, 256], "float32"), "xu": ("sbuf", [128, 256], "float32"),
    "zk": ("sbuf", [128, 256], "float32"), "zu": ("sbuf", [128, 256], "float32"),
    "lstk": ("sbuf", [128, 256], "uint16"), "lstu": ("sbuf", [128, 256], "uint16"),
    "u1i": ("sbuf", [128, 256], "int32"),
    "di": ("sbuf", [128, 1536], "int32"), "db": ("sbuf", [128, 2048], "bfloat16"),
    "pn": ("sbuf", [128, 256], "int32"), "pc3": ("sbuf", [128, 2], "int32"), "adc": ("sbuf", [128, 1], "float32"),
    "pcf": ("sbuf", [128, 1], "float32"),
    "lki": ("sbuf", [128, 64], "int32"), "a0b": ("sbuf", [128, 256], "bfloat16"),
    "swin": ("sbuf", [128, 4096], "bfloat16"), "mwin": ("sbuf", [128, 4096], "bfloat16"),
    "cwin": ("sbuf", [128, 4096], "bfloat16"), "meta": ("sbuf", [128, 4096], "bfloat16"), "bt": ("sbuf", [128, 4096], "bfloat16"),
    "ax0": ("sbuf", [128, 4096], "bfloat16"), "ax1": ("sbuf", [128, 4096], "bfloat16"),
    "p0": ("sbuf", [128, 2048], "float32"), "p1": ("sbuf", [128, 2048], "float32"),
    "gm0": ("sbuf", [128, 2048], "bfloat16"), "gm1": ("sbuf", [128, 2048], "bfloat16"),
    "mg0": ("sbuf", [128, 2048], "bfloat16"), "mg1": ("sbuf", [128, 2048], "bfloat16"),
    "df": ("sbuf", [128, 1024], "bfloat16"), "dabs": ("sbuf", [128, 1024], "bfloat16"),
    "kd": ("sbuf", [128, 1024], "float32"), "kmn": ("sbuf", [128, 768], "float32"),
    "mk0": ("sbuf", [128, 1024], "bfloat16"),
    "xc": ("sbuf", [128, 256], "int32"), "xh": ("sbuf", [128, 256], "int32"), "xy": ("sbuf", [128, 256], "float32"),
    "xw": ("sbuf", [128, 704], "float32"), "xo": ("sbuf", [128, 256], "float32"),
    "y": ("sbuf", [128, 256], "float32"), "yn": ("sbuf", [128, 256], "float32"),
    "pr": ("sbuf", [128, 1024], "float32"), "a2": ("sbuf", [128, 512], "float32"),
    "cl": ("sbuf", [128, 256], "uint16"), "l2": ("sbuf", [128, 256], "uint16"), "ml": ("sbuf", [128, 256], "uint16"),
    "w0": ("sbuf", [128, _n[0]], "float32"), "w1": ("sbuf", [128, _n[0]], "float32"),
    "wi0": ("sbuf", [128, 128], "int32"), "wi1": ("sbuf", [128, 128], "int32"),
    "idf": ("sbuf", [128, 128], "float32"), "idb": ("sbuf", [128, 128], "bfloat16"), "zz": ("sbuf", [128, 128], "float32"),
    "b4": ("sbuf", [128, 32], "float32"), "bqb": ("sbuf", [128, 128], "bfloat16"),
    "wt": ("sbuf", [128, 512], "float32"), "w4": ("sbuf", [128, 8], "float32"),
    "wm": ("sbuf", [128, 56], "float32"), "wmb": ("sbuf", [128, 56], "bfloat16"),
    "cf": ("sbuf", [128, 256], "float32"), "lby": ("sbuf", [128, 256], "float32"), "eqt": ("sbuf", [128, 1024], "float32"),
    "ypt": ("sbuf", [128, 1024], "float32"), "ycs": ("sbuf", [128, 256], "float32"),
    "acc": ("sbuf", [128, 512], "float32"), "fin": ("sbuf", [128, 256], "float32"), "yes": ("sbuf", [128, 256], "float32"),
}
for _k in range(8): SCRATCH["dg%d" % _k] = ("dram", [8, 4096], "bfloat16")
for _k in range(4):
    SCRATCH["ra%d" % _k] = ("sbuf", [128, 256], "bfloat16")
    SCRATCH["rl%d" % _k] = ("sbuf", [128, 64], "uint16")
    SCRATCH["rm%d" % _k] = ("sbuf", [128, 1024], "bfloat16")
    SCRATCH["rE%d" % _k] = ("sbuf", [128, 256], "float32")
    SCRATCH["ms%d" % _k] = ("sbuf", [128, 256], "float32")
for _k in ("pA", "pM", "pN", "pL"):
    for _h in "01": SCRATCH[_k + _h] = ("psum", [128, 512], "float32")

_DS = ["dk", "du", "da", "dl", "da0", "dyk", "dyu", "dxc", "dss", "dmm", "ddg", "dcw", "dm1", "dm2", "dy0", "dyc", "dye0", "dye1"]
SEMAPHORES = ["sv", "ss", "sp", "sg", "rl"] + _DS + ["aA%d" % k for k in range(4)] + ["aL%d" % k for k in range(4)] \
    + ["aM%d" % k for k in range(4)] + ["aE1", "aE2", "aE3a", "aE3b"]


def rank_program(g, core, T, topo):
    me = T.rank_of(core)
    if me is None:
        return
    cores = list(T.cores); N = len(cores)
    peers = [c for c in cores if c != core]
    Q = {"V": g.vector, "S": g.scalar, "P": g.tensor, "G": g, "Y": g.sync}
    SEM = {"V": "sv", "S": "ss", "P": "sp", "G": "sg"}
    cnt = {}; known = {e: {} for e in Q}; snap = {}; lastw = {}; reads = {}; bank = {}

    def need(e, evs):
        best = {}
        for s, v in evs: best[s] = max(best.get(s, 0), v)
        for s in sorted(best, key=lambda k: (k in ("sv", "ss", "sp", "sg"), k)):
            v = best[s]; kn = known[e]
            if kn.get(s, 0) >= v: continue
            Q[e].wait_ge(T.sem[s], v)
            for s2, v2 in snap.get((s, v), {}).items():
                if kn.get(s2, 0) < v2: kn[s2] = v2
            kn[s] = v

    def deps(e, r, w, b, asyn=False):
        evs = []
        for t in r:
            if t in lastw: evs.append(lastw[t])
        for t in w:
            if t in lastw: evs.append(lastw[t])
            for e2, ev in reads.get(t, {}).items():
                if e2 != e or asyn: evs.append(ev)
        for t in b:
            for e2, ev in bank.get(t, {}).items():
                if e2 != e: evs.append(ev)
        need(e, evs)

    def done(e, key, ev, r, w, b):
        snap[ev] = dict(known[e])
        for t in r: reads.setdefault(t, {})[key] = ev
        for t in w:
            lastw[t] = ev; reads[t] = {}
        for t in b: bank.setdefault(t, {})[key] = ev

    def op(e, calls, r=(), w=(), b=()):
        deps(e, r, w, b)
        s = SEM[e]
        for c in (calls if isinstance(calls, list) else [calls]):
            c().then_inc(T.sem[s], 1); cnt[s] = cnt.get(s, 0) + 1
        done(e, e, (s, cnt[s]), r, w, b)

    def dmag(e, pairs, sem, r=(), w=()):
        deps(e, r, w, (), True)
        for o, i in pairs:
            Q[e].dma_start(out=o, in_=i).then_inc(T.sem[sem], 16)
        cnt[sem] = 16 * len(pairs)
        done(e, "dma" + sem, (sem, cnt[sem]), r, w, ())

    def send(src, name, dsts, rsem, r):
        deps("G", r, (), ())
        eng = topo.engines(core, dsts[0][0])
        ids = []
        for c, _x in dsts:
            a = topo.addr(c); ids.append(DstId(rid=a[0], pnc=a[1]))
        g.remote_dma_fused([RemoteDMATransfer(dst_ids=ids, dma_engine_mask=topo.mask(core, dsts[0][0]), remote_sem=T.sem[rsem],
                                              srcs=[src], dsts=[d for _c, d in dsts])], local_sem=T.sem.rl)
        cnt["rl"] = cnt.get("rl", 0) + len(eng)

    def v(n, h, st=0, step=1):
        o, w = _W[n]; return T["w%d" % h][:, o + st:o + w:step]

    def vb(n, h, a, b):
        o, w = _W[n]; return T["w%d" % h][:, o + a:o + b]

    def tk(s, h): return [x + str(h) for x in s.split()]

    def tt(o, a, b, f, h, w, r, bk=""):
        op("V", lambda: g.vector.tensor_tensor(out=o, in0=a, in1=b, op=f), tk(r, h), tk(w, h), tk(bk, h))

    def ts(o, a, s1, s2, f0, f1, r, w, b=()):
        if f1 is None: op("V", lambda: g.vector.tensor_scalar(out=o, in0=a, scalar1=s1, scalar2=None, op0=f0), r, w, b)
        else: op("V", lambda: g.vector.tensor_scalar(out=o, in0=a, scalar1=s1, scalar2=s2, op0=f0, op1=f1), r, w, b)

    def cp(o, a, r, w, b=()):
        op("V", lambda: g.vector.tensor_copy(out=o, in_=a), r, w, b)

    def act(o, a, f, r, w, b=(), bias=0.0, scale=1.0):
        op("S", lambda: g.scalar.activation(out=o, in_=a, func=f, bias=bias, scale=scale), r, w, b)

    def ms(o, c, w):
        op("V", lambda: g.vector.memset(o, c), (), w)

    def mm(o, l, r_, st, sp):
        return lambda: g.tensor.matmul(out=o, lhsT=l, rhs=r_, start=st, stop=sp)

    RA = "ra%d" % me; RL = "rl%d" % me; RM = "rm%d" % me
    ne = len(topo.engines(core, peers[0]))
    for k in range(N):
        if k != me:
            lastw["ra%d" % k] = ("aA%d" % k, ne); lastw["rl%d" % k] = ("aL%d" % k, ne); lastw["rm%d" % k] = ("aM%d" % k, ne)
    lastw["rE1"] = ("aE1", ne); lastw["rE2"] = ("aE2", ne); lastw["rE3h0"] = ("aE3a", ne); lastw["rE3h1"] = ("aE3b", ne)

    dmag("Y", [(T.kl[:, :], T.kid[:, :])], "dk", (), ["kl"])
    dmag("S", [(T[RA][:, :], T.a[:, :])], "da", (), [RA])
    dmag("S", [(T.lki[:, :], T.lk[:, :])], "dl", (), ["lki"])
    dmag("S", [(T.a0b[:, :], T.a0[:, :])], "da0", (), ["a0b"])
    dmag("Y", [(T.ul[:, :], T.up[:, :])], "du", (), ["ul"])
    dmag("Y", [(T.ytk[:, 128 * k:128 * k + 128], T.kid[k::2, :]) for k in (0, 1)], "dyk", (), ["ytk"])
    dmag("Y", [(T.ytu[:, 128 * k:128 * k + 128], T.up[k::2, :]) for k in (0, 1)], "dyu", (), ["ytu"])
    dmag("S", [(T.xc[:, t * 64:t * 64 + 64], T.cut0[t::4, :]) for t in range(4)], "dxc", (), ["xc"])
    dmag("S", [(T.swin[:, :], T.s[:, :])], "dss", (), ["swin"])

    ms(T.b4[:, :], 1.0, ["b4"]); ms(T.zz[:, :], 0.0, ["zz"]); ms(T.wm[:, :], 0.0, ["wm"]); ms(T.w4[:, :], 4.0, ["w4"])
    ms(T.cwin[:, 4080:4096], 0.0, ["cwin"]); ms(T.wt[:, :], 0.0, ["wt"])

    def sel(buf, tok, pat, base, cm, cmp_, fill, src=None, stok=None):
        op("G", lambda: g.affine_select(out=buf, in_=buf if src is None else src, pattern=pat, compare_op=cmp_, fill=fill, base=base,
                                        channel_multiplier=cm), [tok] if stok is None else [stok], [tok])
    op("G", lambda: g.iota(T.pn[:, :], [[0, 256]], 0, 1), (), ["pn"])
    op("G", lambda: g.iota(T.di[:, 1024:1280], [[1, 256]], 0, 0), (), ["di4"])
    sel(T.b4[:, :], "b4", [[-4, 32]], 0, 1, OP.is_ge, 0.0)
    sel(T.b4[:, :], "b4", [[4, 32]], 3, -1, OP.is_ge, 0.0)

    cp(T[RL][:, :], T.lki[:, :], ["lki"], [RL])
    send(T[RA][:, :], RA, [(c, T[RA][:, :]) for c in peers], "aA%d" % me, [RA])
    send(T[RL][:, :], RL, [(c, T[RL][:, :]) for c in peers], "aL%d" % me, [RL])

    sel(T.idf[:, :], "idf", [[-1, 128]], 0, 1, OP.not_equal, 1.0, T.zz[:, :], "zz")
    sel(T.w4[:, :], "w4", [[-16, 8]], 0, 1, OP.is_ge, 0.0)
    sel(T.w4[:, :], "w4", [[16, 8]], 15, -1, OP.is_ge, 0.0)
    TERMS = [(0, 0, 2.0), (0, 1, 512.0), (1, 9, 1.0), (1, 10, 256.0), (2, 11, 1.0), (2, 12, 256.0), (3, 13, 16.0), (3, 14, 4096.0),
             (4, 3, 2.0), (4, 4, 512.0), (4, 5, BIG), (5, 6, 2.0), (5, 7, 512.0), (5, 8, BIG), (6, 13, 16.0), (6, 14, 4096.0), (6, 2, BIG)]
    for o_ in range(7):
        for oo, i_, w_ in TERMS:
            if oo == o_: sel(T.wm[:, oo * 8:oo * 8 + 8], "wm", [[-16, 8]], -i_, 1, OP.not_equal, w_)

    def spread_g(b, ax, rows):
        for r in rows:
            op("G", lambda: g.affine_select(out=T[ax][:, r::16], in_=T["ra%d" % b][:, :], pattern=[[0, 256]], compare_op=OP.is_gt, fill=0.0,
                                            base=1, channel_multiplier=0), ["ra%d" % b], [ax + "r%d" % r])
    spread_g(me, "ax0", range(8, 16))
    for r in range(8):
        act(T.ax0[:, r::16], T[RA][:, :], AF.Copy, [RA], ["ax0r%d" % r])

    ts(T.di[:, 0:256], T.kl[:, :], 1, 255, OP.arith_shift_right, OP.bitwise_and, ["kl"], ["di0"])
    ts(T.di[:, 256:512], T.kl[:, :], 9, None, OP.arith_shift_right, None, ["kl"], ["di1"])
    ts(T.db[:, 1536:1792], T.kl[:, :], 0, None, OP.is_lt, None, ["kl"], ["db6"])
    ts(T.db[:, 1792:2048], T.kl[:, :], 0, None, OP.is_ge, None, ["kl"], ["db7"])
    ts(T.u1i[:, :], T.ul[:, :], 1, None, OP.add, None, ["ul"], ["u1i"])
    ts(T.di[:, 1280:1536], T.pn[:, :], 15, None, OP.bitwise_and, None, ["pn"], ["di5"])
    ts(T.di[:, 512:768], T.u1i[:, :], 255, None, OP.bitwise_and, None, ["u1i"], ["di2"])
    ts(T.di[:, 768:1024], T.u1i[:, :], 8, None, OP.arith_shift_right, None, ["u1i"], ["di3"])
    cp(T.db[:, 0:1536], T.di[:, :], ["di%d" % k for k in range(6)], ["db0"])
    dmag("Y", [(T["dg%d" % k][:, :], T.db[:, 256 * k:256 * k + 256]) for k in range(8)], "ddg", ["db0", "db6", "db7"], ["dg"])
    C = T.cwin
    prs = [(C[i::16, :], T["dg%d" % k][:, :]) for i, k in ((0, 0), (1, 1), (2, 6), (3, 0), (4, 1), (5, 7), (9, 2), (10, 3), (11, 2), (12, 3),
                                                           (13, 4), (14, 5), (15, 4))]
    prs += [(C[i::16, 0:4095], T["dg%d" % k][:, 1:4096]) for i, k in ((6, 0), (7, 1), (8, 7))]
    dmag("Y", prs, "dcw", ["dg"], ["cwin"])
    dmag("Y", [(T.mwin[:, :], T.m[:, :])], "dmm", (), ["mwin"])

    def dist(aw, lkb, mout):
        for k in range(4):
            op("V", lambda: g.vector.tensor_tensor(out=T.df[:, k * 256:k * 256 + 256], in0=T[aw][:, 0:256].indirect(T[lkb][:, 16 * k:16 * k + 16]),
                                                   in1=T[RA][:, :], op=OP.subtract), [aw, lkb, RA], ["df%d" % k])
        for k in range(2):
            act(T.dabs[:, k * 512:k * 512 + 512], T.df[:, k * 512:k * 512 + 512], AF.Abs, ["df%d" % (2 * k), "df%d" % (2 * k + 1)], ["dabs%d" % k])
            op("P", mm(T["pL%d" % k][:, :], T.bqb[:, :], T.dabs[:, k * 512:k * 512 + 512], True, True), ["bqb", "dabs%d" % k], ["dp%d" % k], ["pL%d" % k])
        for k in range(4):
            act(T.kd[:, k * 256:k * 256 + 256], T["pL%d" % (k // 2)][:, (k % 2) * 256:(k % 2) * 256 + 256], AF.Identity, ["dp%d" % (k // 2)],
                ["kd%d" % k], ["pL%d" % (k // 2)], float(k), 4.0)

    def dist2(mout):
        op("V", lambda: g.vector.tensor_tensor(out=T.kmn[:, 0:512], in0=T.kd[:, 0:512], in1=T.kd[:, 512:1024], op=OP.min),
           ["kd0", "kd1", "kd2", "kd3"], ["kmn"])
        op("V", lambda: g.vector.tensor_tensor(out=T.kmn[:, 512:768], in0=T.kmn[:, 0:256], in1=T.kmn[:, 256:512], op=OP.min), ["kmn"], ["kmm"])
        for k in range(4):
            op("V", lambda: g.vector.tensor_tensor(out=T[mout][:, k * 256:k * 256 + 256], in0=T.kd[:, k * 256:k * 256 + 256], in1=T.kmn[:, 512:768],
                                                   op=OP.is_equal), ["kd%d" % k, "kmm"], [mout])

    for k in range(4): cp(T.bqb[:, k::4], T.b4[:, :], ["b4"], ["bqb"])
    dist("a0b", RL, "mk0")

    for yt, x_, z_, ls_ in (("ytk", "xk", "zk", "lstk"), ("ytu", "xu", "zu", "lstu")):
        for b in range(8):
            for k in (0, 1):
                cp(T[x_][:, 32 * b + 16 * k:32 * b + 16 * k + 16], T[yt][:, 128 * k + 16 * b:128 * k + 16 * b + 16], [yt], [x_])
        op("V", lambda: g.vector.transpose(out=T[z_][:, :], in_=T[x_][:, :]), [x_], [z_])
        for b in range(8):
            cp(T[ls_][:, b::8], T[z_][:, 32 * b:32 * b + 32], [z_], [ls_])
    dist2("mk0")
    op("S", lambda: g.scalar.activation(out=T.meta[:, :], in_=T.cwin[:, :].indirect(T.lstk[:, :]), func=AF.Copy), ["cwin", "lstk"], ["meta"])
    op("S", lambda: g.scalar.activation(out=T.bt[:, :], in_=T.cwin[:, :].indirect(T.lstu[:, :]), func=AF.Copy), ["cwin", "lstu"], ["bt"])
    dmag("Y", [(T.meta[i::16, :], T["dg%d" % k][:, :]) for i, k in ((0, 0), (1, 1), (2, 6), (9, 2), (10, 3), (13, 4), (14, 5))], "dm1", ["dg"], ["meta"])

    ts(T.xh[:, :], T.xc[:, :], 1, None, OP.arith_shift_right, None, ["xc"], ["xh"])
    for t in range(4):
        ts(T.xy[:, t * 64:t * 64 + 64], T.xc[:, t * 64:t * 64 + 64], 1.0, (3 - t) / 16.0, OP.mult, OP.add, ["xc"], ["xy%d" % t])

    def xw(k): return T.xw[:, k * 64:k * 64 + 64]

    def xs(b, t): return b[:, t * 64:t * 64 + 64]

    def x2(o, a, b, f, r, w): op("V", lambda: g.vector.tensor_tensor(out=o, in0=a, in1=b, op=f), r, w)
    for k, (i, j) in enumerate(((0, 2), (1, 3), (0, 3), (1, 2))):
        x2(xw(k), xs(T.xh, i), xs(T.xh, j), OP.is_equal, ["xh"], ["xw%d" % k])
    x2(xw(6), xs(T.xy, 2), xs(T.xy, 1), OP.subtract, ["xy1", "xy2"], ["xw6"])
    x2(xw(7), xs(T.xy, 3), xs(T.xy, 1), OP.subtract, ["xy1", "xy3"], ["xw7"])
    x2(xw(4), xw(0), xw(1), OP.max, ["xw0", "xw1"], ["xw4"])
    x2(xw(5), xw(2), xw(3), OP.max, ["xw2", "xw3"], ["xw5"])
    cp(xs(T.xo, 0), xs(T.xy, 0), ["xy0"], ["xo"])
    x2(xw(8), xw(4), xw(6), OP.mult, ["xw4", "xw6"], ["xw8"])
    x2(xw(9), xw(5), xw(7), OP.mult, ["xw5", "xw7"], ["xw9"])
    x2(xw(10), xs(T.xy, 1), xw(8), OP.add, ["xy1", "xw8"], ["xw10"])
    x2(xs(T.xo, 2), xs(T.xy, 2), xw(8), OP.subtract, ["xy2", "xw8"], ["xo"])
    x2(xs(T.xo, 3), xs(T.xy, 3), xw(9), OP.subtract, ["xy3", "xw9"], ["xo"])
    x2(xs(T.xo, 1), xw(10), xw(9), OP.add, ["xw10", "xw9"], ["xo"])
    dmag("Y", [(T.y[t::4, :], T.xo[:, t * 64:t * 64 + 64]) for t in range(4)], "dy0", ["xo"], ["y0", "y1"])
    dmag("Y", [(T.meta[i::16, :], T.bt[i::16, :]) for i in (11, 12)], "dm2", ["bt"], ["meta"])
    cp(T.idb[:, :], T.idf[:, :], ["idf"], ["idb"])
    cp(T.wmb[:, :], T.wm[:, :], ["wm"], ["wmb"])
    ts(T.pc3[:, 0:1], T.pn[:, 0:1], 3, None, OP.bitwise_and, None, ["pn"], ["pc3"])
    ts(T.adc[:, :], T.pc3[:, 0:1], -2, -1, OP.add, OP.max, ["pc3"], ["adc"])

    AXR = lambda h: ["ax%dr%d" % (h % 2, r) for r in range(16)]

    def pmx(o_, h, st=0, step=1): return T["pM%d" % h][:, o_ * 128 + st:o_ * 128 + 128:step]

    def pnx(o_, h, st=0, step=1): return T["pN%d" % h][:, o_ * 128 + st:o_ * 128 + 128:step]

    def gather_mul(h, lst, tok, vis, w):
        op("V", lambda: g.vector.tensor_tensor(out=T["p%d" % h][:, :], in0=T.swin[:, :].indirect(T[lst][:, h * 128:h * 128 + 128]),
                                               in1=T["ax%d" % (vis % 2)][:, h * 2048:h * 2048 + 2048], op=OP.mult),
           ["swin", tok + str(h)] + AXR(vis), ["p%d" % h])

    def dots(h, col, w):
        op("P", [mm(T["pA%d" % h][:, col + r:col + 128:16], T["p%d" % h][:, r::16], T.w4[:, :], True, True) for r in range(16)],
           ["p%d" % h, "w4"], [w + str(h)], ["pA%d" % h])

    def meta_mm(h):
        op("P", mm(pnx(3, h), T.yn[:, h * 128:h * 128 + 128], T.idf[:, :], True, True), ["yn%d" % h, "idf"], ["yd%d" % h], ["pN%d" % h])
        cl = []
        for r in range(16):
            cl.append(mm(T["pM%d" % h][:, r::16], T["gm%d" % h][:, r::16], T.wmb[:, 0:32], True, True))
            cl.append(mm(T["pN%d" % h][:, r:384:16], T["gm%d" % h][:, r::16], T.wmb[:, 32:56], True, True))
        op("P", cl, ["gm%d" % h, "wmb"], ["m%d" % h, "n%d" % h], ["pM%d" % h, "pN%d" % h])

    def s_copies(h):
        act(v("ups", h), pmx(1, h), AF.Copy, tk("m", h), tk("ups", h), ["pM%d" % h])
        act(v("yd16", h), pnx(3, h), AF.Identity, tk("yd", h), tk("yd16", h), ["pN%d" % h], 0.0, 16.0)

    def off_a(h):
        tt(v("lab", h), v("yd16", h), pmx(3, h), OP.subtract, h, "lab", "yd16 m", "pM")
        tt(v("eq", h), v("ups", h, 0, 2), pmx(1, h, 1, 2), OP.is_equal, h, "eq", "ups m", "pM")
        tt(v("lbk", h), v("yd16", h), pnx(2, h), OP.subtract, h, "lbk", "yd16 n", "pN")
        tt(v("peq", h), v("eq", h), pmx(1, h, 0, 2), OP.mult, h, "peq", "eq m", "pM")
        tt(v("xa", h), v("lab", h, 0, 2), v("lab", h, 1, 2), OP.max, h, "xa", "lab")
        tt(v("na", h), v("lab", h, 0, 2), v("lab", h, 1, 2), OP.min, h, "na", "lab")

    def dec1(h):
        tt(v("kes", h), v("lbk", h), T["pA%d" % h][:, 0:128], OP.add, h, "kes", "lbk ke", "pA")
        e, o = v("kes", h, 0, 2), v("kes", h, 1, 2)
        tt(v("mab", h), e, o, OP.max, h, "mab", "kes")
        tt(v("w1", h), o, e, OP.is_gt, h, "w1", "kes")
        tt(v("w0", h), e, o, OP.is_gt, h, "w0", "kes")
        A, B = v("mab", h, 0, 2), v("mab", h, 1, 2)
        tt(v("sab", h, 0, 2), A, B, OP.is_gt, h, "sA", "mab")
        tt(v("sab", h, 1, 2), B, A, OP.is_gt, h, "sB", "mab")
        tt(v("o", h, 0, 2), v("sab", h), v("w0", h), OP.mult, h, "oe", "sA sB w0")
        tt(v("o", h, 1, 2), v("sab", h), v("w1", h), OP.mult, h, "oo", "sA sB w1")
        sA, sB = v("sab", h, 0, 2), v("sab", h, 1, 2)
        tt(v("pa", h), sB, v("peq", h, 0, 2), OP.mult, h, "pa", "sB peq")
        tt(v("pb", h), sA, v("peq", h, 1, 2), OP.mult, h, "pb", "sA peq")
        tt(v("prk", h), v("o", h), pmx(0, h), OP.mult, h, "prk", "oe oo m", "pM")
        tt(v("ga", h), sB, pmx(2, h, 0, 4), OP.mult, h, "ga", "sB m", "pM")
        tt(v("gb", h), sA, pmx(2, h, 2, 4), OP.mult, h, "gb", "sA m", "pM")
        tt(v("t1", h), v("prk", h, 0, 2), v("prk", h, 1, 2), OP.add, h, "t1", "prk")
        tt(v("lt", h, 0, 4), v("pa", h), v("pb", h), OP.add, h, "lta", "pa pb")
        tt(v("lt", h, 1, 4), v("ga", h), v("gb", h), OP.add, h, "ltb", "ga gb")
        tt(v("lt", h, 2, 4), v("t1", h, 0, 2), v("t1", h, 1, 2), OP.add, h, "ltc", "t1")
        tt(v("lt", h, 3, 4), v("t1", h, 0, 2), v("t1", h, 1, 2), OP.add, h, "ltd", "t1")
        op("P", mm(T["pL%d" % h][:, 0:128], v("lt", h), T.idf[:, :], True, True), tk("lta ltb ltc ltd", h) + ["idf"], tk("plt", h), ["pL%d" % h])

    def conv(h):
        ts(T.l2[:, h * 128:h * 128 + 128], T["pL%d" % h][:, 0:128], T.adc[:, 0:1], None, OP.add, None, tk("plt", h) + ["adc"], tk("l2", h), ["pL%d" % h])

    def off_b1(h):
        sA, sB = v("sab", h, 0, 2), v("sab", h, 1, 2)
        tt(v("nab", h), v("kes", h, 0, 2), v("kes", h, 1, 2), OP.min, h, "nab", "kes")
        tt(vb("mk", h, 0, 32), v("mab", h, 0, 2), v("mab", h, 1, 2), OP.max, h, "mka", "mab")
        tt(v("ja", h), sB, v("xa", h, 0, 2), OP.mult, h, "ja", "sB xa")
        tt(v("jb", h), sA, v("xa", h, 1, 2), OP.mult, h, "jb", "sA xa")
        tt(v("pa2", h), sB, v("na", h, 0, 2), OP.mult, h, "pa2", "sB na")
        tt(v("pb2", h), sA, v("na", h, 1, 2), OP.mult, h, "pb2", "sA na")
        tt(v("ka", h), sA, v("nab", h, 0, 2), OP.mult, h, "ka", "sA nab")
        tt(v("kb", h), sB, v("nab", h, 1, 2), OP.mult, h, "kb", "sB nab")
        tt(v("lj", h), v("ja", h), v("jb", h), OP.add, h, "lj", "ja jb")
        tt(v("ljp", h), v("pa2", h), v("pb2", h), OP.add, h, "ljp", "pa2 pb2")
        tt(vb("mk", h, 32, 64), v("ka", h), v("kb", h), OP.add, h, "mkb", "ka kb")
        tt(v("prl", h), v("o", h), pnx(0, h), OP.mult, h, "prl", "oe oo n", "pN")
        tt(v("prr", h), v("o", h), pnx(1, h), OP.mult, h, "prr", "oe oo n", "pN")
        wi = T["wi%d" % h]
        cp(wi[:, 0:64], v("mk", h), tk("mka mkb", h), tk("mki", h))
        tt(v("u1", h), v("o", h, 1, 2), pmx(1, h, 0, 2), OP.mult, h, "u1", "oo m", "pM")
        tt(v("u2", h), v("o", h, 0, 2), pmx(1, h, 1, 2), OP.mult, h, "u2", "oe m", "pM")
        ts(wi[:, 64:128], wi[:, 0:64], 3, None, OP.bitwise_and, None, tk("mki", h), tk("mkj", h))
        tt(v("y1", h), v("o", h, 1, 2), pnx(3, h, 0, 2), OP.mult, h, "y1t", "oo yd", "pN")
        tt(v("y2", h), v("o", h, 0, 2), pnx(3, h, 1, 2), OP.mult, h, "y2t", "oe yd", "pN")
        cp(v("lbf", h), wi[:, 64:128], tk("mkj", h), tk("lbf", h))
        tt(v("tl", h), v("prl", h, 0, 2), v("prl", h, 1, 2), OP.add, h, "tl", "prl")
        tt(v("tr", h), v("prr", h, 0, 2), v("prr", h, 1, 2), OP.add, h, "tr", "prr")
        tt(v("u3", h), v("u1", h), v("u2", h), OP.add, h, "u3", "u1 u2")
        tt(v("y3", h), v("y1", h), v("y2", h), OP.add, h, "y3", "y1t y2t")
        tt(vb("z", h, 0, 32), v("tl", h, 0, 2), v("tl", h, 1, 2), OP.add, h, "za", "tl")
        tt(vb("z", h, 32, 64), v("tr", h, 0, 2), v("tr", h, 1, 2), OP.add, h, "zb", "tr")
        tt(v("mx", h), v("lj", h), vb("lbf", h, 32, 64), OP.max, h, "mx", "lj lbf")
        tt(v("mn", h), v("lj", h), vb("lbf", h, 32, 64), OP.min, h, "mn", "lj lbf")
        tt(v("upu", h), v("u3", h, 0, 2), v("u3", h, 1, 2), OP.add, h, "upu", "u3")
        tt(v("s1", h, 1, 4), v("y3", h, 0, 2), v("y3", h, 1, 2), OP.add, h, "s1b", "y3")
        ts(v("hasp", h), v("lt", h, 0, 4), 0.0, None, OP.is_gt, None, tk("lta", h), tk("hasp", h))
        tt(v("sib", h), v("upu", h), v("lt", h, 1, 4), OP.is_equal, h, "sib", "upu ltb")
        c = 1.0 / 16.0
        act(v("ljm", h), v("lj", h), AF.Identity, tk("lj", h), tk("ljm", h), (), -1.0, c)
        act(v("ljq", h), v("ljp", h), AF.Identity, tk("ljp", h), tk("ljq", h), (), 1.0, c)
        act(v("lp", h), v("ljp", h), AF.Identity, tk("ljp", h), tk("lp", h), (), 0.0, c)
        act(v("ls", h), vb("lbf", h, 0, 32), AF.Identity, tk("lbf", h), tk("ls", h), (), 0.0, c)
        act(v("zc", h), v("z", h), AF.Relu, tk("za zb", h), tk("zc", h), (), -BIG, 1.0)
        act(v("mxm", h), v("mx", h), AF.Identity, tk("mx", h), tk("mxm", h), (), -1.0, c)
        act(v("mn1", h), v("mn", h), AF.Identity, tk("mn", h), tk("mn1", h), (), 1.0, c)

    def off_b2(h):
        za, zb = vb("zc", h, 0, 32), vb("zc", h, 32, 64)
        tt(v("s1", h, 0, 4), v("lt", h, 0, 4), v("ljm", h), OP.add, h, "s1a", "lta ljm")
        tt(v("s1", h, 2, 4), v("lt", h, 2, 4), v("ls", h), OP.add, h, "s1c", "ltc ls")
        tt(v("s1", h, 3, 4), v("lt", h, 3, 4), v("ljq", h), OP.add, h, "s1d", "ltd ljq")
        tt(v("aa", h), za, v("ls", h), OP.add, h, "aa", "zc ls")
        tt(v("bb", h), zb, v("lp", h), OP.add, h, "bb", "zc lp")
        tt(v("dz", h), za, zb, OP.subtract, h, "dz", "zc")
        tt(v("s2", h, 0, 4), v("lt", h, 1, 4), v("mxm", h), OP.add, h, "s2a", "ltb mxm")
        tt(v("zr1", h), zb, v("mn1", h), OP.add, h, "zr1", "zc mn1")
        tt(v("dab", h), v("aa", h), v("bb", h), OP.subtract, h, "dab", "aa bb")
        tt(v("dr", h), v("s1", h, 3, 4), v("s1", h, 2, 4), OP.subtract, h, "dr", "s1c s1d")

    def dec2(h):
        def F(k): return T["pA%d" % h][:, 128 + k:256:4]
        ls, M, KU = vb("lbf", h, 0, 32), vb("mk", h, 0, 32), vb("mk", h, 32, 64)
        pa = ["pA%d" % h]
        tt(v("fk2", h), ls, F(2), OP.add, h, "fk2", "lbf f", "pA")
        tt(v("fk3", h), v("ljp", h), F(3), OP.add, h, "fk3", "ljp f", "pA")
        tt(v("fk0", h), v("lj", h), F(0), OP.add, h, "fk0", "lj f", "pA")
        ts(v("d0", h), F(0), 3.0, None, OP.add, None, tk("f", h), tk("d0", h), pa)
        ts(v("d1", h), F(1), 3.0, None, OP.add, None, tk("f", h), tk("d1", h), pa)
        tt(v("kl", h), v("fk2", h), vb("z", h, 0, 32), OP.min, h, "klt", "fk2 za")
        tt(v("kr", h), v("fk3", h), vb("z", h, 32, 64), OP.min, h, "krt", "fk3 zb")
        tt(v("mxu", h), v("fk0", h), KU, OP.max, h, "mxu", "fk0 mkb")
        tt(v("g1a", h), M, v("d0", h), OP.is_gt, h, "g1a", "mka d0")
        tt(v("k2", h), v("kl", h), v("kr", h), OP.max, h, "k2", "klt krt")
        tt(v("sl", h), v("kl", h), v("kr", h), OP.is_gt, h, "sl", "klt krt")
        tt(v("g1", h), v("g1a", h), v("hasp", h), OP.mult, h, "g1", "g1a hasp")
        tt(v("b1", h), v("k2", h), v("mxu", h), OP.is_gt, h, "b1", "k2 mxu")
        tt(v("b2", h), v("k2", h), v("d1", h), OP.is_gt, h, "b2", "k2 d1")
        tt(v("e1", h), v("sl", h), v("dr", h), OP.mult, h, "e1", "sl dr")
        tt(v("e2", h), v("sl", h), v("dab", h), OP.mult, h, "e2", "sl dab")
        tt(v("gs", h), v("g1", h), v("sib", h), OP.mult, h, "gs", "g1 sib")
        tt(v("bbb", h), v("b1", h), v("b2", h), OP.mult, h, "bbb", "b1 b2")
        ts(v("m0", h), v("g1", h), -1.0, 1.0, OP.mult, OP.add, tk("g1", h), tk("m0", h))
        tt(v("e3", h), v("sl", h), v("dz", h), OP.mult, h, "e3", "sl dz")
        tt(v("go2", h), v("bbb", h), v("gs", h), OP.mult, h, "go2", "bbb gs")
        tt(v("s2", h, 1, 4), v("s1", h, 2, 4), v("e1", h), OP.add, h, "s2b", "s1c e1")
        tt(v("s2", h, 2, 4), v("bb", h), v("e2", h), OP.add, h, "s2c", "bb e2")
        tt(v("s2", h, 3, 4), v("zr1", h), v("e3", h), OP.add, h, "s2d", "zr1 e3")
        for k in range(4): tt(v("n0", h, k, 4), v("m0", h), pnx(3, h, k, 4), OP.mult, h, "n0" + "abcd"[k], "m0 yd", "pN")
        tt(v("m1", h), v("g1", h), v("go2", h), OP.subtract, h, "m1", "g1 go2")
        for k in range(4): tt(v("n2", h, k, 4), v("go2", h), v("s2", h, k, 4), OP.mult, h, "n2" + "abcd"[k], "go2 s2" + "abcd"[k])
        for k in range(4): tt(v("n1", h, k, 4), v("m1", h), v("s1", h, k, 4), OP.mult, h, "n1" + "abcd"[k], "m1 s1" + "abcd"[k])
        for j, n in enumerate(("n0", "n2", "n1")):
            op("P", mm(T["pL%d" % h][:, 128:256], v(n, h), T.idf[:, :], j == 0, j == 2), tk(" ".join(n + x for x in "abcd"), h) + ["idf"],
               tk("pnn", h), ["pL%d" % h])

    def keep(h):
        cp(T.ml[:, h * 128:h * 128 + 128], T["pL%d" % h][:, 128:256], tk("pnn", h), tk("ml", h), ["pL%d" % h])
        cp(T.y[:, h * 128:h * 128 + 128], T["pL%d" % h][:, 128:256], tk("pnn", h), tk("y", h), ["pL%d" % h])

    def m_gather(h, e):
        if e == "S":
            op("S", lambda: g.scalar.activation(out=T["mg%d" % h][:, :], in_=T.mwin[:, :].indirect(T.ml[:, h * 128:h * 128 + 128]), func=AF.Copy),
               ["mwin"] + tk("ml", h), tk("mg", h))
        else:
            op("V", lambda: g.vector.tensor_copy(out=T["mg%d" % h][:, :], in_=T.mwin[:, :].indirect(T.ml[:, h * 128:h * 128 + 128])),
               ["mwin"] + tk("ml", h), tk("mg", h))

    def m_sum(h):
        op("P", [mm(T["pL%d" % h][:, 256:384], T.idb[:, :], T["mg%d" % h][:, r::16], r == 0, r == 15) for r in range(16)],
           tk("mg", h) + ["idb"], tk("pms", h), ["pL%d" % h])

    def m_out(h, vis):
        act(T["ms%d" % vis][:, h * 128:h * 128 + 128], T["pL%d" % h][:, 256:384], AF.Copy, tk("pms", h), ["ms%dh%d" % (vis, h)], ["pL%d" % h])

    def m_send(vis):
        c = cores[(me - vis) % N]
        if vis in (1, 2):
            send(T["ms%d" % vis][:, :], "", [(c, T["rE%d" % vis][:, :])], "aE%d" % vis, ["ms%dh0" % vis, "ms%dh1" % vis])
        if vis == 3:
            for h in (0, 1):
                send(T.ms3[:, h * 128:h * 128 + 128], "", [(c, T.rE3[:, h * 128:h * 128 + 128])], "aE3" + "ab"[h], ["ms3h%d" % h])

    for vis in range(4):
        b = (me - vis) % N
        mk = "mk0" if vis == 0 else "rm%d" % b
        lk = "rl%d" % b
        op("V", lambda: g.vector.tensor_tensor(out=T.pr[:, :], in0=T.y[:, 0:256].indirect(T[lk][:, 0:64]), in1=T[mk][:, :], op=OP.mult),
           ["y0", "y1", lk, mk], ["pr"])
        op("V", lambda: g.vector.tensor_tensor(out=T.a2[:, :], in0=T.pr[:, 0:512], in1=T.pr[:, 512:1024], op=OP.add), ["pr"], ["a2"])
        for h in (0, 1):
            op("V", lambda: g.vector.tensor_tensor(out=T.yn[:, h * 128:h * 128 + 128], in0=T.a2[:, h * 128:h * 128 + 128],
                                                   in1=T.a2[:, 256 + h * 128:384 + h * 128], op=OP.add), ["a2"], ["yn%d" % h])
        for h in (0, 1):
            cp(T.cl[:, h * 128:h * 128 + 128], T.yn[:, h * 128:h * 128 + 128], ["yn%d" % h], ["cl%d" % h])
        for h in (0, 1):
            op("S", lambda: g.scalar.activation(out=T["gm%d" % h][:, :], in_=T.meta[:, :].indirect(T.cl[:, h * 128:h * 128 + 128]), func=AF.Copy),
               ["meta", "cl%d" % h], ["gm%d" % h])
            gather_mul(h, "cl", "cl", vis, "")
        if vis == 0: dist("ra%d" % ((me + 1) % N), RL, RM)
        for h in (0, 1):
            meta_mm(h)
            dots(h, 0, "ke")
        for h in (0, 1): s_copies(h)
        if vis == 0:
            dist2(RM)
            spread_g((me - 1) % N, "ax1", range(16))
            send(T[RM][:, :], RM, [(c, T[RM][:, :]) for c in peers], "aM%d" % me, [RM])
        if vis > 0:
            m_gather(0, "S"); m_gather(1, "S")
        for h in (0, 1):
            off_a(h); dec1(h)
        for h in (0, 1):
            conv(h); gather_mul(h, "l2", "l2", vis, "")
        for h in (0, 1):
            dots(h, 128, "f")
        if vis in (0, 1): spread_g((me - vis - 2) % N, "ax%d" % (vis % 2), range(16))
        if vis > 0:
            m_sum(0); m_sum(1)
        for h in (0, 1): off_b1(h)
        if vis > 0:
            m_out(0, vis - 1); m_out(1, vis - 1)
            m_send(vis - 1)
        for h in (0, 1):
            off_b2(h); dec2(h)
        for h in (0, 1): keep(h)

    m_gather(0, "S"); m_gather(1, "V")
    m_sum(0); m_out(0, 3)
    for t in range(4): cp(T.wt[:, t * 128 + t:(t + 1) * 128:4], T.b4[:, :], ["b4", "wt"], ["wt%d" % t])
    cp(T.cf[:, :], T.ml[:, :], ["ml0", "ml1"], ["cf"])
    m_sum(1); m_out(1, 3); m_send(3)
    op("V", lambda: g.vector.tensor_tensor(out=T.lby[:, :], in0=T.y[:, :], in1=T.cf[:, :], op=OP.subtract), ["y0", "y1", "cf"], ["lby"])
    for t in range(4):
        ts(T.eqt[:, t * 256:t * 256 + 256], T.lby[:, :], (3 - t) / 16.0, None, OP.is_equal, None, ["lby"], ["eqt%d" % t])
    for t in range(4):
        op("V", lambda: g.vector.tensor_tensor(out=T.ypt[:, t * 256:t * 256 + 256], in0=T.eqt[:, t * 256:t * 256 + 256], in1=T.cf[:, :], op=OP.mult),
           ["eqt%d" % t, "cf"], ["ypt%d" % t])
        op("P", mm(T.pN0[:, 0:256], T.wt[:, t * 128:t * 128 + 128], T.ypt[:, t * 256:t * 256 + 256], t == 0, t == 3), ["wt%d" % t, "ypt%d" % t],
           ["pyc"], ["pN0"])
    op("V", lambda: g.vector.tensor_tensor(out=T.acc[:, 0:256], in0=T.ms0[:, :], in1=T.rE1[:, :], op=OP.add), ["ms0h0", "ms0h1", "rE1"], ["acc0"])
    cp(T.ycs[:, :], T.pN0[:, 0:256], ["pyc"], ["ycs"], ["pN0"])
    dmag("Y", [(T.yc[:, :], T.ycs[:, :])], "dyc", ["ycs"], ["yc"])
    op("V", lambda: g.vector.tensor_tensor(out=T.acc[:, 256:512], in0=T.acc[:, 0:256], in1=T.rE2[:, :], op=OP.add), ["acc0", "rE2"], ["acc1"])
    for h in (0, 1):
        c = slice(h * 128, h * 128 + 128)
        op("V", lambda: g.vector.tensor_tensor(out=T.fin[:, c], in0=T.acc[:, 256 + h * 128:384 + h * 128], in1=T.rE3[:, c], op=OP.add),
           ["acc1", "rE3h%d" % h], ["fin%d" % h])
        op("V", lambda: g.vector.tensor_tensor(out=T.yes[:, c], in0=T.fin[:, c], in1=T[RA][:, c], op=OP.mult), ["fin%d" % h, RA], ["yes%d" % h])
        dmag("Y", [(T.ye[:, c], T.yes[:, c])], "dye%d" % h, ["yes%d" % h], ["ye%d" % h])

    need("G", [(s, cnt[s]) for s in cnt])
